import numpy as np
import ml_dtypes


def mxq(x, axis, fmt="e4m3"):
    dtype, down = {"e4m3": (ml_dtypes.float8_e4m3fn, 7), "e5m2": (ml_dtypes.float8_e5m2, 14)}[fmt]
    v = np.moveaxis(np.asarray(x, np.float32).astype(ml_dtypes.bfloat16).astype(np.float64), axis, -1)
    blocks = v.reshape(v.shape[:-1] + (-1, 32))
    amax = np.abs(blocks).max(-1, keepdims=True)
    byte = np.maximum(np.where(amax > 0, np.frexp(amax)[1] - 1 + 127, 0) - down, 1)
    scale = np.exp2(byte - 127.0)
    codes = (blocks / scale).astype(np.float32).astype(dtype).astype(np.float64)
    return np.moveaxis((codes * scale).reshape(v.shape), -1, axis)


WIDE = False


def mx_kscale(k):
    if not WIDE:
        return np.ones(k)
    levels = np.array([10, -10, 5, -5, 0])
    if k % 512:
        return np.exp2(np.random.permutation(np.resize(levels, k // 32))).repeat(32)
    a = np.empty((k // 512, 16))
    for p in range(k // 512):
        a[p, :8] = np.random.permutation(np.resize(levels, 8))
        for g in range(8):
            far = levels[np.abs(levels - a[p, g]) >= 10]
            a[p, g + 8] = far[np.random.randint(len(far))]
    return np.exp2(a.ravel()).repeat(32)


def f64(x):
    return np.asarray(x).astype(np.float64)


def striped(idx):
    return np.tile(idx.reshape(-1, 16).T, (8, 1)).astype(np.uint16)


def unstriped(offs):
    return offs[:16].T.reshape(-1).astype(np.int64)


def pack_weight(w):
    k, n = w.shape
    w = f64(np.asarray(w, np.float32).astype(ml_dtypes.bfloat16)).reshape(k // 32, 32, n)
    amax = np.abs(w).max(1)
    byte = np.clip(np.where(amax > 0, np.frexp(amax)[1] - 1 + 127 - 7, 1), 1, 254)
    scaled = (w * np.exp2(127.0 - byte)[:, None, :]).reshape(k, n).astype(np.float32)
    words = np.ascontiguousarray(scaled.reshape(k // 512, 128, 4, n).transpose(0, 1, 3, 2)).astype(ml_dtypes.float8_e4m3fn).view(np.uint8)
    return words, np.ascontiguousarray(byte.astype(np.uint8).reshape(k // 512, 16, n))


def unpack_weight(words, scales):
    g, p, n, _ = words.shape
    vals = np.ascontiguousarray(words).view(ml_dtypes.float8_e4m3fn).astype(np.float64) * np.repeat(np.exp2(scales.astype(np.float64) - 127.0), 8, axis=1)[..., None]
    return vals.transpose(0, 1, 3, 2).reshape(g * 512, n)


K, T, S, N = 512, 4096, 1024, 512


def setup_inputs():
    n = np.random.standard_normal
    s = mx_kscale(K)[:, None]
    w1, w2 = n((2, K, N)) / np.sqrt(2 * K) / s[None]
    packed = pack_weight(n((K, T)) * s)
    return {
        "xT": (n((K, S)) * s).astype(np.float32),
        "s_words": packed[0],
        "s_scales": packed[1],
        "w1": w1.astype(np.float32),
        "w2": w2.astype(np.float32),
        "offs": striped(np.random.permutation(T)[:S]),
    }


def reference(xT, s_words, s_scales, w1, w2, offs):
    y = mxq(f64(w1), 0, "e4m3").T @ mxq(f64(xT), 0, "e4m3") + mxq(f64(w2), 0, "e4m3").T @ unpack_weight(s_words, s_scales)[:, unstriped(offs)]
    return y

@@ -1,0 +1,151 @@
+from contextlib import ExitStack
+
+import concourse.mybir as mybir
+
+K, T, S, M = 512, 4096, 1024, 512
+FLOPS = 2 * 2 * K * M * S
+
+F32 = mybir.dt.float32
+BF16 = mybir.dt.bfloat16
+I32 = mybir.dt.int32
+U32 = mybir.dt.uint32
+U16 = mybir.dt.uint16
+U8 = mybir.dt.uint8
+FP8X4 = mybir.dt.float8_e4m3fn_x4
+
+P = 128
+PACK = 4
+M_TILE = 128
+M_TILES = M // M_TILE
+CHUNK = 256
+CHUNKS = S // CHUNK
+HALF = 512
+RUN = 4
+
+
+def interleave(copy, grouped, raw):
+    copy(
+        grouped.rearrange("p (c i) t -> p c t i", i=RUN),
+        raw.rearrange("p t (c i) -> p c t i", i=RUN),
+    )
+
+
+def quantize(nc, codes, scales, grouped):
+    nc.vector.quantize_mx(
+        out=codes.bitcast(FP8X4),
+        scales=scales,
+        in_=grouped.rearrange("p c t -> p (c t)"),
+    )
+
+
+def tile_picked_recall_none_p_kernel(tc, xT, s_words, s_scales, w1, w2, offs, out):
+    nc = tc.nc
+    with ExitStack() as ctx:
+        keep = ctx.enter_context(tc.tile_pool(name="keep", bufs=1))
+        psum = ctx.enter_context(tc.psum_pool(name="psum", bufs=8))
+
+        offsets = keep.tile([P, S // 16], U16, name="offsets")
+        store_words = keep.tile([P, T], U32, name="store_words", align_bytes=64)
+        store_scales = keep.tile([P, T], U8, name="store_scales", align_bytes=64)
+        w2_raw = keep.tile([P, PACK, M], F32, name="w2_raw", align_bytes=64)
+        w1_raw = [keep.tile([P, PACK, CHUNK], F32, name=f"w1_raw{h}", align_bytes=64) for h in range(2)]
+        x_raw = [keep.tile([P, PACK, CHUNK], F32, name=f"x_raw{c}", align_bytes=64) for c in range(CHUNKS)]
+
+        nc.vector.memset(store_scales[:].bitcast(I32), 0)
+        for r in range(4):
+            nc.gpsimd.dma_start(out=store_scales[r:P:32, :].bitcast(I32), in_=s_scales[0, r:16:4, :].bitcast(I32))
+
+        w1_rows = w1.rearrange("(p t) m -> p t m", t=PACK)
+        x_rows = xT.rearrange("(p t) j -> p t j", t=PACK)
+        nc.sync.dma_start(out=w2_raw[:], in_=w2.rearrange("(p t) m -> p t m", t=PACK))
+        nc.sync.dma_start(offsets[:], offs)
+        nc.sync.dma_start(out=store_words[:].bitcast(I32), in_=s_words[0].rearrange("p n t -> p (n t)").bitcast(I32))
+        for h in range(2):
+            nc.sync.dma_start(out=w1_raw[h][:], in_=w1_rows[:, :, h * CHUNK : (h + 1) * CHUNK])
+        for c in range(CHUNKS):
+            nc.sync.dma_start(out=x_raw[c][:], in_=x_rows[:, :, c * CHUNK : (c + 1) * CHUNK])
+
+        w2_bf = keep.tile([P, M, PACK], BF16, name="w2_bf", align_bytes=64)
+        w2_codes = keep.tile([P, M], U32, name="w2_codes", align_bytes=64)
+        w2_scales = keep.tile([P, M], U8, name="w2_scales", align_bytes=64)
+        w1_bf = keep.tile([P, M, PACK], BF16, name="w1_bf", align_bytes=64)
+        w1_codes = keep.tile([P, M], U32, name="w1_codes", align_bytes=64)
+        w1_scales = keep.tile([P, M], U8, name="w1_scales", align_bytes=64)
+        x_bf = keep.tile([P, S, PACK], BF16, name="x_bf", align_bytes=64)
+        x_codes = keep.tile([P, S], U32, name="x_codes", align_bytes=64)
+        x_scales = keep.tile([P, S], U8, name="x_scales", align_bytes=64)
+        mem_words = keep.tile([P, S], U32, name="mem_words", align_bytes=64)
+        mem_scales = keep.tile([P, S], U8, name="mem_scales", align_bytes=64)
+
+        lo, hi = slice(0, CHUNK), slice(CHUNK, M)
+        interleave(nc.vector.tensor_copy, w2_bf[:, lo, :], w2_raw[:, :, lo])
+        interleave(nc.scalar.copy, w2_bf[:, hi, :], w2_raw[:, :, hi])
+        quantize(nc, w2_codes[:, lo], w2_scales[:, lo], w2_bf[:, lo, :])
+        quantize(nc, w2_codes[:, hi], w2_scales[:, hi], w2_bf[:, hi, :])
+
+        nc.vector.tensor_copy(mem_scales[:], store_scales[:].indirect(offsets[:]))
+        for h in range(S // HALF):
+            nc.vector.tensor_copy(
+                mem_words[:, h * HALF : (h + 1) * HALF],
+                store_words[:].indirect(offsets[:, h * HALF // 16 : (h + 1) * HALF // 16]),
+            )
+
+        for h, cols in enumerate((lo, hi)):
+            interleave(nc.scalar.copy, w1_bf[:, cols, :], w1_raw[h][:])
+            quantize(nc, w1_codes[:, cols], w1_scales[:, cols], w1_bf[:, cols, :])
+
+        banks = {}
+
+        def open_groups(c):
+            cols = slice(c * CHUNK, (c + 1) * CHUNK)
+            for m in range(M_TILES):
+                rows = slice(m * M_TILE, (m + 1) * M_TILE)
+                banks[c, m] = psum.tile([M_TILE, CHUNK], F32, name="acc")
+                nc.tensor.matmul_mx(
+                    out=banks[c, m][:],
+                    lhsT=w2_codes[:, rows].bitcast(FP8X4),
+                    lhsT_scale=w2_scales[:, rows],
+                    rhs=mem_words[:, cols].bitcast(FP8X4),
+                    rhs_scale=mem_scales[:, cols],
+                    start=True,
+                    stop=False,
+                )
+
+        def quantize_queries(c):
+            parts = [slice(q * 128, (q + 1) * 128) for q in range(2)]
+            for q in parts:
+                cols = slice(c * CHUNK + q.start, c * CHUNK + q.stop)
+                interleave(nc.vector.tensor_copy, x_bf[:, cols, :], x_raw[c][:, :, q])
+            for q in parts:
+                cols = slice(c * CHUNK + q.start, c * CHUNK + q.stop)
+                quantize(nc, x_codes[:, cols], x_scales[:, cols], x_bf[:, cols, :])
+
+        out_rows = out.rearrange("(m p) j -> p m j", p=M_TILE)
+
+        def finish(c):
+            cols = slice(c * CHUNK, (c + 1) * CHUNK)
+            result = keep.tile([M_TILE, M_TILES, CHUNK], F32, name=f"result{c}", align_bytes=64)
+            for m in range(M_TILES):
+                rows = slice(m * M_TILE, (m + 1) * M_TILE)
+                nc.tensor.matmul_mx(
+                    out=banks[c, m][:],
+                    lhsT=w1_codes[:, rows].bitcast(FP8X4),
+                    lhsT_scale=w1_scales[:, rows],
+                    rhs=x_codes[:, cols].bitcast(FP8X4),
+                    rhs_scale=x_scales[:, cols],
+                    start=False,
+                    stop=True,
+                )
+                if c == CHUNKS - 1 and m % 2 == 1:
+                    nc.vector.tensor_copy(result[:, m, :], banks[c, m][:])
+                else:
+                    nc.scalar.copy(result[:, m, :], banks[c, m][:])
+            nc.sync.dma_start(out=out_rows[:, :, cols], in_=result[:])
+
+        open_groups(0)
+        open_groups(1)
+        for c in range(CHUNKS):
+            quantize_queries(c)
+            finish(c)
+            if c + 2 < CHUNKS:
+                open_groups(c + 2)

@@ -51,9 +51,13 @@ def tile_picked_recall_none_p_kernel(tc, xT, s_words, s_scales, w1, w2, offs, ou
         w1_raw = [keep.tile([P, PACK, CHUNK], F32, name=f"w1_raw{h}", align_bytes=64) for h in range(2)]
         x_raw = [keep.tile([P, PACK, CHUNK], F32, name=f"x_raw{c}", align_bytes=64) for c in range(CHUNKS)]
 
-        nc.vector.memset(store_scales[:].bitcast(I32), 0)
+        landed_scales = keep.tile([P, T], U8, name="landed_scales", align_bytes=64)
         for r in range(4):
-            nc.gpsimd.dma_start(out=store_scales[r:P:32, :].bitcast(I32), in_=s_scales[0, r:16:4, :].bitcast(I32))
+            nc.sync.dma_start(out=landed_scales[r:P:32, :].bitcast(I32), in_=s_scales[0, r:16:4, :].bitcast(I32))
+        nc.vector.memset(store_scales[:].bitcast(I32), 0)
+        for q in range(4):
+            live = slice(32 * q, 32 * q + 4)
+            nc.vector.tensor_copy(store_scales[live, :].bitcast(I32), landed_scales[live, :].bitcast(I32))
 
         w1_rows = w1.rearrange("(p t) m -> p t m", t=PACK)
         x_rows = xT.rearrange("(p t) j -> p t j", t=PACK)
@@ -78,12 +82,9 @@ def tile_picked_recall_none_p_kernel(tc, xT, s_words, s_scales, w1, w2, offs, ou
         mem_scales = keep.tile([P, S], U8, name="mem_scales", align_bytes=64)
 
         lo, hi = slice(0, CHUNK), slice(CHUNK, M)
-        interleave(nc.vector.tensor_copy, w2_bf[:, lo, :], w2_raw[:, :, lo])
-        interleave(nc.scalar.copy, w2_bf[:, hi, :], w2_raw[:, :, hi])
-        quantize(nc, w2_codes[:, lo], w2_scales[:, lo], w2_bf[:, lo, :])
-        quantize(nc, w2_codes[:, hi], w2_scales[:, hi], w2_bf[:, hi, :])
-
         nc.vector.tensor_copy(mem_scales[:], store_scales[:].indirect(offsets[:]))
+        interleave(nc.scalar.copy, w2_bf[:], w2_raw[:])
+        quantize(nc, w2_codes[:], w2_scales[:], w2_bf[:])
         for h in range(S // HALF):
             nc.vector.tensor_copy(
                 mem_words[:, h * HALF : (h + 1) * HALF],
@@ -140,7 +141,8 @@ def tile_picked_recall_none_p_kernel(tc, xT, s_words, s_scales, w1, w2, offs, ou
                     nc.vector.tensor_copy(result[:, m, :], banks[c, m][:])
                 else:
                     nc.scalar.copy(result[:, m, :], banks[c, m][:])
-            nc.sync.dma_start(out=out_rows[:, :, cols], in_=result[:])
+                if m % 2 == 1:
+                    nc.sync.dma_start(out=out_rows[:, m - 1 : m + 1, cols], in_=result[:, m - 1 : m + 1, :])
 
         open_groups(0)
         open_groups(1)

@@ -20,14 +20,10 @@ M_TILES = M // M_TILE
 CHUNK = 256
 CHUNKS = S // CHUNK
 HALF = 512
-RUN = 4
 
 
 def interleave(copy, grouped, raw):
-    copy(
-        grouped.rearrange("p (c i) t -> p c t i", i=RUN),
-        raw.rearrange("p t (c i) -> p c t i", i=RUN),
-    )
+    copy(grouped, raw.rearrange("p t c -> p c t"))
 
 
 def quantize(nc, codes, scales, grouped):
@@ -61,12 +57,13 @@ def tile_picked_recall_none_p_kernel(tc, xT, s_words, s_scales, w1, w2, offs, ou
 
         w1_rows = w1.rearrange("(p t) m -> p t m", t=PACK)
         x_rows = xT.rearrange("(p t) j -> p t j", t=PACK)
-        nc.sync.dma_start(out=w2_raw[:], in_=w2.rearrange("(p t) m -> p t m", t=PACK))
         nc.sync.dma_start(offsets[:], offs)
+        nc.sync.dma_start(out=w2_raw[:], in_=w2.rearrange("(p t) m -> p t m", t=PACK))
         nc.sync.dma_start(out=store_words[:].bitcast(I32), in_=s_words[0].rearrange("p n t -> p (n t)").bitcast(I32))
-        for h in range(2):
-            nc.sync.dma_start(out=w1_raw[h][:], in_=w1_rows[:, :, h * CHUNK : (h + 1) * CHUNK])
-        for c in range(CHUNKS):
+        nc.sync.dma_start(out=w1_raw[0][:], in_=w1_rows[:, :, 0:CHUNK])
+        nc.sync.dma_start(out=x_raw[0][:], in_=x_rows[:, :, 0:CHUNK])
+        nc.sync.dma_start(out=w1_raw[1][:], in_=w1_rows[:, :, CHUNK:M])
+        for c in range(1, CHUNKS):
             nc.sync.dma_start(out=x_raw[c][:], in_=x_rows[:, :, c * CHUNK : (c + 1) * CHUNK])
 
         w2_bf = keep.tile([P, M, PACK], BF16, name="w2_bf", align_bytes=64)
@@ -81,7 +78,6 @@ def tile_picked_recall_none_p_kernel(tc, xT, s_words, s_scales, w1, w2, offs, ou
         mem_words = keep.tile([P, S], U32, name="mem_words", align_bytes=64)
         mem_scales = keep.tile([P, S], U8, name="mem_scales", align_bytes=64)
 
-        lo, hi = slice(0, CHUNK), slice(CHUNK, M)
         nc.vector.tensor_copy(mem_scales[:], store_scales[:].indirect(offsets[:]))
         interleave(nc.scalar.copy, w2_bf[:], w2_raw[:])
         quantize(nc, w2_codes[:], w2_scales[:], w2_bf[:])
@@ -91,9 +87,14 @@ def tile_picked_recall_none_p_kernel(tc, xT, s_words, s_scales, w1, w2, offs, ou
                 store_words[:].indirect(offsets[:, h * HALF // 16 : (h + 1) * HALF // 16]),
             )
 
-        for h, cols in enumerate((lo, hi)):
-            interleave(nc.scalar.copy, w1_bf[:, cols, :], w1_raw[h][:])
-            quantize(nc, w1_codes[:, cols], w1_scales[:, cols], w1_bf[:, cols, :])
+        interleave(nc.scalar.copy, w1_bf[:, 0:CHUNK, :], w1_raw[0][:])
+        quantize(nc, w1_codes[:, 0:CHUNK], w1_scales[:, 0:CHUNK], w1_bf[:, 0:CHUNK, :])
+        interleave(nc.vector.tensor_copy, x_bf[:, 0:128, :], x_raw[0][:, :, 0:128])
+        interleave(nc.scalar.copy, x_bf[:, 128:CHUNK, :], x_raw[0][:, :, 128:CHUNK])
+        quantize(nc, x_codes[:, 0:CHUNK], x_scales[:, 0:CHUNK], x_bf[:, 0:CHUNK, :])
+        interleave(nc.vector.tensor_copy, w1_bf[:, CHUNK : CHUNK + 128, :], w1_raw[1][:, :, 0:128])
+        interleave(nc.scalar.copy, w1_bf[:, CHUNK + 128 : M, :], w1_raw[1][:, :, 128:CHUNK])
+        quantize(nc, w1_codes[:, CHUNK:M], w1_scales[:, CHUNK:M], w1_bf[:, CHUNK:M, :])
 
         banks = {}
 
@@ -146,8 +147,9 @@ def tile_picked_recall_none_p_kernel(tc, xT, s_words, s_scales, w1, w2, offs, ou
 
         open_groups(0)
         open_groups(1)
-        for c in range(CHUNKS):
+        finish(0)
+        for c in range(1, CHUNKS):
             quantize_queries(c)
+            if c >= 2:
+                open_groups(c)
             finish(c)
-            if c + 2 < CHUNKS:
-                open_groups(c + 2)

@@ -23,7 +23,7 @@ HALF = 512
 
 
 def interleave(copy, grouped, raw):
-    copy(grouped, raw.rearrange("p t c -> p c t"))
+    copy(grouped.rearrange("p (c i) t -> p c t i", i=2), raw.rearrange("p t (c i) -> p c t i", i=2))
 
 
 def quantize(nc, codes, scales, grouped):
@@ -50,6 +50,8 @@ def tile_picked_recall_none_p_kernel(tc, xT, s_words, s_scales, w1, w2, offs, ou
         landed_scales = keep.tile([P, T], U8, name="landed_scales", align_bytes=64)
         for r in range(4):
             nc.sync.dma_start(out=landed_scales[r:P:32, :].bitcast(I32), in_=s_scales[0, r:16:4, :].bitcast(I32))
+            if r == 1:
+                nc.sync.dma_start(offsets[:], offs)
         nc.vector.memset(store_scales[:].bitcast(I32), 0)
         for q in range(4):
             live = slice(32 * q, 32 * q + 4)
@@ -57,13 +59,13 @@ def tile_picked_recall_none_p_kernel(tc, xT, s_words, s_scales, w1, w2, offs, ou
 
         w1_rows = w1.rearrange("(p t) m -> p t m", t=PACK)
         x_rows = xT.rearrange("(p t) j -> p t j", t=PACK)
-        nc.sync.dma_start(offsets[:], offs)
         nc.sync.dma_start(out=w2_raw[:], in_=w2.rearrange("(p t) m -> p t m", t=PACK))
         nc.sync.dma_start(out=store_words[:].bitcast(I32), in_=s_words[0].rearrange("p n t -> p (n t)").bitcast(I32))
         nc.sync.dma_start(out=w1_raw[0][:], in_=w1_rows[:, :, 0:CHUNK])
         nc.sync.dma_start(out=x_raw[0][:], in_=x_rows[:, :, 0:CHUNK])
+        nc.sync.dma_start(out=x_raw[1][:], in_=x_rows[:, :, CHUNK : 2 * CHUNK])
         nc.sync.dma_start(out=w1_raw[1][:], in_=w1_rows[:, :, CHUNK:M])
-        for c in range(1, CHUNKS):
+        for c in range(2, CHUNKS):
             nc.sync.dma_start(out=x_raw[c][:], in_=x_rows[:, :, c * CHUNK : (c + 1) * CHUNK])
 
         w2_bf = keep.tile([P, M, PACK], BF16, name="w2_bf", align_bytes=64)
@@ -87,69 +89,79 @@ def tile_picked_recall_none_p_kernel(tc, xT, s_words, s_scales, w1, w2, offs, ou
                 store_words[:].indirect(offsets[:, h * HALF // 16 : (h + 1) * HALF // 16]),
             )
 
-        interleave(nc.scalar.copy, w1_bf[:, 0:CHUNK, :], w1_raw[0][:])
-        quantize(nc, w1_codes[:, 0:CHUNK], w1_scales[:, 0:CHUNK], w1_bf[:, 0:CHUNK, :])
-        interleave(nc.vector.tensor_copy, x_bf[:, 0:128, :], x_raw[0][:, :, 0:128])
-        interleave(nc.scalar.copy, x_bf[:, 128:CHUNK, :], x_raw[0][:, :, 128:CHUNK])
-        quantize(nc, x_codes[:, 0:CHUNK], x_scales[:, 0:CHUNK], x_bf[:, 0:CHUNK, :])
-        interleave(nc.vector.tensor_copy, w1_bf[:, CHUNK : CHUNK + 128, :], w1_raw[1][:, :, 0:128])
-        interleave(nc.scalar.copy, w1_bf[:, CHUNK + 128 : M, :], w1_raw[1][:, :, 128:CHUNK])
-        quantize(nc, w1_codes[:, CHUNK:M], w1_scales[:, CHUNK:M], w1_bf[:, CHUNK:M, :])
+        def prepare(bf, codes, scales, first, raw, scalar_share):
+            share = CHUNK - scalar_share
+            cuts = [0, share] if share <= 128 else [0, 128, share]
+            for a, b in zip(cuts, cuts[1:]):
+                if b > a:
+                    interleave(nc.vector.tensor_copy, bf[:, first + a : first + b, :], raw[:, :, a:b])
+            if scalar_share:
+                interleave(nc.scalar.copy, bf[:, first + share : first + CHUNK, :], raw[:, :, share:CHUNK])
+            width = 128 if share > 128 else CHUNK
+            for a in range(first, first + CHUNK, width):
+                quantize(nc, codes[:, a : a + width], scales[:, a : a + width], bf[:, a : a + width, :])
 
-        banks = {}
-
-        def open_groups(c):
+        def memory_pass(bank, c, m):
             cols = slice(c * CHUNK, (c + 1) * CHUNK)
-            for m in range(M_TILES):
-                rows = slice(m * M_TILE, (m + 1) * M_TILE)
-                banks[c, m] = psum.tile([M_TILE, CHUNK], F32, name="acc")
-                nc.tensor.matmul_mx(
-                    out=banks[c, m][:],
-                    lhsT=w2_codes[:, rows].bitcast(FP8X4),
-                    lhsT_scale=w2_scales[:, rows],
-                    rhs=mem_words[:, cols].bitcast(FP8X4),
-                    rhs_scale=mem_scales[:, cols],
-                    start=True,
-                    stop=False,
-                )
+            rows = slice(m * M_TILE, (m + 1) * M_TILE)
+            nc.tensor.matmul_mx(
+                out=bank,
+                lhsT=w2_codes[:, rows].bitcast(FP8X4),
+                lhsT_scale=w2_scales[:, rows],
+                rhs=mem_words[:, cols].bitcast(FP8X4),
+                rhs_scale=mem_scales[:, cols],
+                start=True,
+                stop=False,
+            )
 
-        def quantize_queries(c):
-            parts = [slice(q * 128, (q + 1) * 128) for q in range(2)]
-            for q in parts:
-                cols = slice(c * CHUNK + q.start, c * CHUNK + q.stop)
-                interleave(nc.vector.tensor_copy, x_bf[:, cols, :], x_raw[c][:, :, q])
-            for q in parts:
-                cols = slice(c * CHUNK + q.start, c * CHUNK + q.stop)
-                quantize(nc, x_codes[:, cols], x_scales[:, cols], x_bf[:, cols, :])
+        def query_pass(bank, c, m):
+            cols = slice(c * CHUNK, (c + 1) * CHUNK)
+            rows = slice(m * M_TILE, (m + 1) * M_TILE)
+            nc.tensor.matmul_mx(
+                out=bank,
+                lhsT=w1_codes[:, rows].bitcast(FP8X4),
+                lhsT_scale=w1_scales[:, rows],
+                rhs=x_codes[:, cols].bitcast(FP8X4),
+                rhs_scale=x_scales[:, cols],
+                start=False,
+                stop=True,
+            )
 
         out_rows = out.rearrange("(m p) j -> p m j", p=M_TILE)
 
-        def finish(c):
-            cols = slice(c * CHUNK, (c + 1) * CHUNK)
-            result = keep.tile([M_TILE, M_TILES, CHUNK], F32, name=f"result{c}", align_bytes=64)
-            for m in range(M_TILES):
-                rows = slice(m * M_TILE, (m + 1) * M_TILE)
-                nc.tensor.matmul_mx(
-                    out=banks[c, m][:],
-                    lhsT=w1_codes[:, rows].bitcast(FP8X4),
-                    lhsT_scale=w1_scales[:, rows],
-                    rhs=x_codes[:, cols].bitcast(FP8X4),
-                    rhs_scale=x_scales[:, cols],
-                    start=False,
-                    stop=True,
-                )
-                if c == CHUNKS - 1 and m % 2 == 1:
-                    nc.vector.tensor_copy(result[:, m, :], banks[c, m][:])
-                else:
-                    nc.scalar.copy(result[:, m, :], banks[c, m][:])
-                if m % 2 == 1:
-                    nc.sync.dma_start(out=out_rows[:, m - 1 : m + 1, cols], in_=result[:, m - 1 : m + 1, :])
+        def store(c, m, result):
+            nc.sync.dma_start(out=out_rows[:, m : m + 2, c * CHUNK : (c + 1) * CHUNK], in_=result[:])
 
-        open_groups(0)
-        open_groups(1)
-        finish(0)
-        for c in range(1, CHUNKS):
-            quantize_queries(c)
-            if c >= 2:
-                open_groups(c)
-            finish(c)
+        def shared_block(c, m):
+            bank = psum.tile([M_TILE, 2, CHUNK], F32, name="acc")
+            result = keep.tile([M_TILE, 2, CHUNK], F32, name=f"result{c}{m}", align_bytes=64)
+            for i in range(2):
+                memory_pass(bank[:, i, :], c, m + i)
+                query_pass(bank[:, i, :], c, m + i)
+            nc.scalar.copy(result[:], bank[:])
+            store(c, m, result)
+
+        def split_block(c, m, second_copy):
+            banks = [psum.tile([M_TILE, CHUNK], F32, name="acc") for i in range(2)]
+            result = keep.tile([M_TILE, 2, CHUNK], F32, name=f"result{c}{m}", align_bytes=64)
+            for i in range(2):
+                memory_pass(banks[i][:], c, m + i)
+            for i, copy in enumerate((nc.scalar.copy, second_copy)):
+                query_pass(banks[i][:], c, m + i)
+                copy(result[:, i, :], banks[i][:])
+            store(c, m, result)
+
+        prepare(w1_bf, w1_codes, w1_scales, 0, w1_raw[0], CHUNK)
+        prepare(x_bf, x_codes, x_scales, 0, x_raw[0], 128)
+        prepare(x_bf, x_codes, x_scales, CHUNK, x_raw[1], 128)
+        shared_block(0, 0)
+        prepare(w1_bf, w1_codes, w1_scales, CHUNK, w1_raw[1], 64)
+        shared_block(1, 0)
+        prepare(x_bf, x_codes, x_scales, 2 * CHUNK, x_raw[2], 0)
+        split_block(0, 2, nc.scalar.copy)
+        shared_block(1, 2)
+        prepare(x_bf, x_codes, x_scales, 3 * CHUNK, x_raw[3], 0)
+        split_block(2, 0, nc.scalar.copy)
+        shared_block(2, 2)
+        split_block(3, 0, nc.vector.tensor_copy)
+        split_block(3, 2, nc.vector.tensor_copy)

@@ -49,8 +49,9 @@ def tile_picked_recall_none_p_kernel(tc, xT, s_words, s_scales, w1, w2, offs, ou
 
         landed_scales = keep.tile([P, T], U8, name="landed_scales", align_bytes=64)
         for r in range(4):
-            nc.sync.dma_start(out=landed_scales[r:P:32, :].bitcast(I32), in_=s_scales[0, r:16:4, :].bitcast(I32))
-            if r == 1:
+            queue = nc.scalar if r % 2 else nc.sync
+            queue.dma_start(out=landed_scales[r:P:32, :].bitcast(I32), in_=s_scales[0, r:16:4, :].bitcast(I32))
+            if r == 2:
                 nc.sync.dma_start(offsets[:], offs)
         nc.vector.memset(store_scales[:].bitcast(I32), 0)
         for q in range(4):
@@ -101,8 +102,7 @@ def tile_picked_recall_none_p_kernel(tc, xT, s_words, s_scales, w1, w2, offs, ou
             for a in range(first, first + CHUNK, width):
                 quantize(nc, codes[:, a : a + width], scales[:, a : a + width], bf[:, a : a + width, :])
 
-        def memory_pass(bank, c, m):
-            cols = slice(c * CHUNK, (c + 1) * CHUNK)
+        def memory_pass(bank, cols, m):
             rows = slice(m * M_TILE, (m + 1) * M_TILE)
             nc.tensor.matmul_mx(
                 out=bank,
@@ -114,8 +114,7 @@ def tile_picked_recall_none_p_kernel(tc, xT, s_words, s_scales, w1, w2, offs, ou
                 stop=False,
             )
 
-        def query_pass(bank, c, m):
-            cols = slice(c * CHUNK, (c + 1) * CHUNK)
+        def query_pass(bank, cols, m):
             rows = slice(m * M_TILE, (m + 1) * M_TILE)
             nc.tensor.matmul_mx(
                 out=bank,
@@ -127,6 +126,9 @@ def tile_picked_recall_none_p_kernel(tc, xT, s_words, s_scales, w1, w2, offs, ou
                 stop=True,
             )
 
+        def chunk(c):
+            return slice(c * CHUNK, (c + 1) * CHUNK)
+
         out_rows = out.rearrange("(m p) j -> p m j", p=M_TILE)
 
         def store(c, m, result):
@@ -136,8 +138,8 @@ def tile_picked_recall_none_p_kernel(tc, xT, s_words, s_scales, w1, w2, offs, ou
             bank = psum.tile([M_TILE, 2, CHUNK], F32, name="acc")
             result = keep.tile([M_TILE, 2, CHUNK], F32, name=f"result{c}{m}", align_bytes=64)
             for i in range(2):
-                memory_pass(bank[:, i, :], c, m + i)
-                query_pass(bank[:, i, :], c, m + i)
+                memory_pass(bank[:, i, :], chunk(c), m + i)
+                query_pass(bank[:, i, :], chunk(c), m + i)
             nc.scalar.copy(result[:], bank[:])
             store(c, m, result)
 
@@ -145,10 +147,21 @@ def tile_picked_recall_none_p_kernel(tc, xT, s_words, s_scales, w1, w2, offs, ou
             banks = [psum.tile([M_TILE, CHUNK], F32, name="acc") for i in range(2)]
             result = keep.tile([M_TILE, 2, CHUNK], F32, name=f"result{c}{m}", align_bytes=64)
             for i in range(2):
-                memory_pass(banks[i][:], c, m + i)
+                memory_pass(banks[i][:], chunk(c), m + i)
             for i, copy in enumerate((nc.scalar.copy, second_copy)):
-                query_pass(banks[i][:], c, m + i)
+                query_pass(banks[i][:], chunk(c), m + i)
                 copy(result[:, i, :], banks[i][:])
+            store(c, m, result)
+
+        def halved_block(c, m, second_copy):
+            result = keep.tile([M_TILE, 2, CHUNK], F32, name=f"result{c}{m}", align_bytes=64)
+            for h, copy in enumerate((nc.scalar.copy, second_copy)):
+                bank = psum.tile([M_TILE, 2, 128], F32, name="acc")
+                cols = slice(c * CHUNK + h * 128, c * CHUNK + (h + 1) * 128)
+                for i in range(2):
+                    memory_pass(bank[:, i, :], cols, m + i)
+                    query_pass(bank[:, i, :], cols, m + i)
+                copy(result[:, :, h * 128 : (h + 1) * 128], bank[:])
             store(c, m, result)
 
         prepare(w1_bf, w1_codes, w1_scales, 0, w1_raw[0], CHUNK)
@@ -161,7 +174,7 @@ def tile_picked_recall_none_p_kernel(tc, xT, s_words, s_scales, w1, w2, offs, ou
         split_block(0, 2, nc.scalar.copy)
         shared_block(1, 2)
         prepare(x_bf, x_codes, x_scales, 3 * CHUNK, x_raw[3], 0)
-        split_block(2, 0, nc.scalar.copy)
+        halved_block(2, 0, nc.scalar.copy)
         shared_block(2, 2)
-        split_block(3, 0, nc.vector.tensor_copy)
+        halved_block(3, 0, nc.vector.tensor_copy)
         split_block(3, 2, nc.vector.tensor_copy)

@@ -62,8 +62,8 @@ def tile_picked_recall_none_p_kernel(tc, xT, s_words, s_scales, w1, w2, offs, ou
         x_rows = xT.rearrange("(p t) j -> p t j", t=PACK)
         nc.sync.dma_start(out=w2_raw[:], in_=w2.rearrange("(p t) m -> p t m", t=PACK))
         nc.sync.dma_start(out=store_words[:].bitcast(I32), in_=s_words[0].rearrange("p n t -> p (n t)").bitcast(I32))
-        nc.sync.dma_start(out=w1_raw[0][:], in_=w1_rows[:, :, 0:CHUNK])
         nc.sync.dma_start(out=x_raw[0][:], in_=x_rows[:, :, 0:CHUNK])
+        nc.sync.dma_start(out=w1_raw[0][:], in_=w1_rows[:, :, 0:CHUNK])
         nc.sync.dma_start(out=x_raw[1][:], in_=x_rows[:, :, CHUNK : 2 * CHUNK])
         nc.sync.dma_start(out=w1_raw[1][:], in_=w1_rows[:, :, CHUNK:M])
         for c in range(2, CHUNKS):
@@ -98,7 +98,7 @@ def tile_picked_recall_none_p_kernel(tc, xT, s_words, s_scales, w1, w2, offs, ou
                     interleave(nc.vector.tensor_copy, bf[:, first + a : first + b, :], raw[:, :, a:b])
             if scalar_share:
                 interleave(nc.scalar.copy, bf[:, first + share : first + CHUNK, :], raw[:, :, share:CHUNK])
-            width = 128 if share > 128 else CHUNK
+            width = 128 if share > 128 or bf is w1_bf else CHUNK
             for a in range(first, first + CHUNK, width):
                 quantize(nc, codes[:, a : a + width], scales[:, a : a + width], bf[:, a : a + width, :])
 
@@ -164,9 +164,9 @@ def tile_picked_recall_none_p_kernel(tc, xT, s_words, s_scales, w1, w2, offs, ou
                 copy(result[:, :, h * 128 : (h + 1) * 128], bank[:])
             store(c, m, result)
 
-        prepare(w1_bf, w1_codes, w1_scales, 0, w1_raw[0], CHUNK)
-        prepare(x_bf, x_codes, x_scales, 0, x_raw[0], 128)
-        prepare(x_bf, x_codes, x_scales, CHUNK, x_raw[1], 128)
+        prepare(x_bf, x_codes, x_scales, 0, x_raw[0], CHUNK)
+        prepare(w1_bf, w1_codes, w1_scales, 0, w1_raw[0], 128)
+        prepare(x_bf, x_codes, x_scales, CHUNK, x_raw[1], 64)
         shared_block(0, 0)
         prepare(w1_bf, w1_codes, w1_scales, CHUNK, w1_raw[1], 64)
         shared_block(1, 0)

@@ -44,7 +44,7 @@ def tile_picked_recall_none_p_kernel(tc, xT, s_words, s_scales, w1, w2, offs, ou
         store_words = keep.tile([P, T], U32, name="store_words", align_bytes=64)
         store_scales = keep.tile([P, T], U8, name="store_scales", align_bytes=64)
         w2_raw = keep.tile([P, PACK, M], F32, name="w2_raw", align_bytes=64)
-        w1_raw = [keep.tile([P, PACK, CHUNK], F32, name=f"w1_raw{h}", align_bytes=64) for h in range(2)]
+        w1_raw = keep.tile([P, PACK, M], F32, name="w1_raw", align_bytes=64)
         x_raw = [keep.tile([P, PACK, CHUNK], F32, name=f"x_raw{c}", align_bytes=64) for c in range(CHUNKS)]
 
         landed_scales = keep.tile([P, T], U8, name="landed_scales", align_bytes=64)
@@ -62,11 +62,8 @@ def tile_picked_recall_none_p_kernel(tc, xT, s_words, s_scales, w1, w2, offs, ou
         x_rows = xT.rearrange("(p t) j -> p t j", t=PACK)
         nc.sync.dma_start(out=w2_raw[:], in_=w2.rearrange("(p t) m -> p t m", t=PACK))
         nc.sync.dma_start(out=store_words[:].bitcast(I32), in_=s_words[0].rearrange("p n t -> p (n t)").bitcast(I32))
-        nc.sync.dma_start(out=x_raw[0][:], in_=x_rows[:, :, 0:CHUNK])
-        nc.sync.dma_start(out=w1_raw[0][:], in_=w1_rows[:, :, 0:CHUNK])
-        nc.sync.dma_start(out=x_raw[1][:], in_=x_rows[:, :, CHUNK : 2 * CHUNK])
-        nc.sync.dma_start(out=w1_raw[1][:], in_=w1_rows[:, :, CHUNK:M])
-        for c in range(2, CHUNKS):
+        nc.sync.dma_start(out=w1_raw[:], in_=w1_rows)
+        for c in range(CHUNKS):
             nc.sync.dma_start(out=x_raw[c][:], in_=x_rows[:, :, c * CHUNK : (c + 1) * CHUNK])
 
         w2_bf = keep.tile([P, M, PACK], BF16, name="w2_bf", align_bytes=64)
@@ -164,17 +161,13 @@ def tile_picked_recall_none_p_kernel(tc, xT, s_words, s_scales, w1, w2, offs, ou
                 copy(result[:, :, h * 128 : (h + 1) * 128], bank[:])
             store(c, m, result)
 
-        prepare(x_bf, x_codes, x_scales, 0, x_raw[0], CHUNK)
-        prepare(w1_bf, w1_codes, w1_scales, 0, w1_raw[0], 128)
-        prepare(x_bf, x_codes, x_scales, CHUNK, x_raw[1], 64)
-        shared_block(0, 0)
-        prepare(w1_bf, w1_codes, w1_scales, CHUNK, w1_raw[1], 64)
-        shared_block(1, 0)
-        prepare(x_bf, x_codes, x_scales, 2 * CHUNK, x_raw[2], 0)
-        split_block(0, 2, nc.scalar.copy)
-        shared_block(1, 2)
-        prepare(x_bf, x_codes, x_scales, 3 * CHUNK, x_raw[3], 0)
-        halved_block(2, 0, nc.scalar.copy)
-        shared_block(2, 2)
+        prepare(w1_bf, w1_codes, w1_scales, 0, w1_raw[:, :, 0:CHUNK], 0)
+        interleave(nc.scalar.copy, w1_bf[:, CHUNK:M, :], w1_raw[:, :, CHUNK:M])
+        prepare(x_bf, x_codes, x_scales, 0, x_raw[0], 96)
+        quantize(nc, w1_codes[:, CHUNK:M], w1_scales[:, CHUNK:M], w1_bf[:, CHUNK:M, :])
+        for c in range(CHUNKS - 1):
+            prepare(x_bf, x_codes, x_scales, (c + 1) * CHUNK, x_raw[c + 1], 96 if c == 0 else 0)
+            halved_block(c, 0, nc.scalar.copy)
+            shared_block(c, 2)
         halved_block(3, 0, nc.vector.tensor_copy)
         split_block(3, 2, nc.vector.tensor_copy)

@@ -38,7 +38,7 @@ def tile_picked_recall_none_p_kernel(tc, xT, s_words, s_scales, w1, w2, offs, ou
     nc = tc.nc
     with ExitStack() as ctx:
         keep = ctx.enter_context(tc.tile_pool(name="keep", bufs=1))
-        psum = ctx.enter_context(tc.psum_pool(name="psum", bufs=8))
+        psum = ctx.enter_context(tc.psum_pool(name="psum", bufs=1))
 
         offsets = keep.tile([P, S // 16], U16, name="offsets")
         store_words = keep.tile([P, T], U32, name="store_words", align_bytes=64)
@@ -131,8 +131,8 @@ def tile_picked_recall_none_p_kernel(tc, xT, s_words, s_scales, w1, w2, offs, ou
         def store(c, m, result):
             nc.sync.dma_start(out=out_rows[:, m : m + 2, c * CHUNK : (c + 1) * CHUNK], in_=result[:])
 
-        def shared_block(c, m):
-            bank = psum.tile([M_TILE, 2, CHUNK], F32, name="acc")
+        def shared_block(c, m, b):
+            bank = psum.tile([M_TILE, 2, CHUNK], F32, name=f"bank{b}")
             result = keep.tile([M_TILE, 2, CHUNK], F32, name=f"result{c}{m}", align_bytes=64)
             for i in range(2):
                 memory_pass(bank[:, i, :], chunk(c), m + i)
@@ -140,8 +140,8 @@ def tile_picked_recall_none_p_kernel(tc, xT, s_words, s_scales, w1, w2, offs, ou
             nc.scalar.copy(result[:], bank[:])
             store(c, m, result)
 
-        def split_block(c, m, second_copy):
-            banks = [psum.tile([M_TILE, CHUNK], F32, name="acc") for i in range(2)]
+        def split_block(c, m, pair, second_copy):
+            banks = [psum.tile([M_TILE, CHUNK], F32, name=f"bank{b}") for b in pair]
             result = keep.tile([M_TILE, 2, CHUNK], F32, name=f"result{c}{m}", align_bytes=64)
             for i in range(2):
                 memory_pass(banks[i][:], chunk(c), m + i)
@@ -150,10 +150,10 @@ def tile_picked_recall_none_p_kernel(tc, xT, s_words, s_scales, w1, w2, offs, ou
                 copy(result[:, i, :], banks[i][:])
             store(c, m, result)
 
-        def halved_block(c, m, second_copy):
+        def halved_block(c, m, pair, second_copy):
             result = keep.tile([M_TILE, 2, CHUNK], F32, name=f"result{c}{m}", align_bytes=64)
             for h, copy in enumerate((nc.scalar.copy, second_copy)):
-                bank = psum.tile([M_TILE, 2, 128], F32, name="acc")
+                bank = psum.tile([M_TILE, 2, 128], F32, name=f"bank{pair[h]}")
                 cols = slice(c * CHUNK + h * 128, c * CHUNK + (h + 1) * 128)
                 for i in range(2):
                     memory_pass(bank[:, i, :], cols, m + i)
@@ -165,9 +165,14 @@ def tile_picked_recall_none_p_kernel(tc, xT, s_words, s_scales, w1, w2, offs, ou
         interleave(nc.scalar.copy, w1_bf[:, CHUNK:M, :], w1_raw[:, :, CHUNK:M])
         prepare(x_bf, x_codes, x_scales, 0, x_raw[0], 96)
         quantize(nc, w1_codes[:, CHUNK:M], w1_scales[:, CHUNK:M], w1_bf[:, CHUNK:M, :])
-        for c in range(CHUNKS - 1):
-            prepare(x_bf, x_codes, x_scales, (c + 1) * CHUNK, x_raw[c + 1], 96 if c == 0 else 0)
-            halved_block(c, 0, nc.scalar.copy)
-            shared_block(c, 2)
-        halved_block(3, 0, nc.vector.tensor_copy)
-        split_block(3, 2, nc.vector.tensor_copy)
+        prepare(x_bf, x_codes, x_scales, CHUNK, x_raw[1], 96)
+        split_block(0, 0, (0, 1), nc.scalar.copy)
+        shared_block(0, 2, 2)
+        prepare(x_bf, x_codes, x_scales, 2 * CHUNK, x_raw[2], 0)
+        split_block(1, 0, (3, 4), nc.scalar.copy)
+        shared_block(1, 2, 5)
+        prepare(x_bf, x_codes, x_scales, 3 * CHUNK, x_raw[3], 0)
+        halved_block(2, 0, (0, 1), nc.scalar.copy)
+        shared_block(2, 2, 6)
+        halved_block(3, 0, (3, 4), nc.vector.tensor_copy)
+        split_block(3, 2, (7, 2), nc.vector.tensor_copy)

@@ -129,7 +129,8 @@ def tile_picked_recall_none_p_kernel(tc, xT, s_words, s_scales, w1, w2, offs, ou
         out_rows = out.rearrange("(m p) j -> p m j", p=M_TILE)
 
         def store(c, m, result):
-            nc.sync.dma_start(out=out_rows[:, m : m + 2, c * CHUNK : (c + 1) * CHUNK], in_=result[:])
+            queue = nc.scalar if (c, m) == (CHUNKS - 1, 2) else nc.sync
+            queue.dma_start(out=out_rows[:, m : m + 2, c * CHUNK : (c + 1) * CHUNK], in_=result[:])
 
         def shared_block(c, m, b):
             bank = psum.tile([M_TILE, 2, CHUNK], F32, name=f"bank{b}")
@@ -168,7 +169,7 @@ def tile_picked_recall_none_p_kernel(tc, xT, s_words, s_scales, w1, w2, offs, ou
         prepare(x_bf, x_codes, x_scales, CHUNK, x_raw[1], 96)
         split_block(0, 0, (0, 1), nc.scalar.copy)
         shared_block(0, 2, 2)
-        prepare(x_bf, x_codes, x_scales, 2 * CHUNK, x_raw[2], 0)
+        prepare(x_bf, x_codes, x_scales, 2 * CHUNK, x_raw[2], 48)
         split_block(1, 0, (3, 4), nc.scalar.copy)
         shared_block(1, 2, 5)
         prepare(x_bf, x_codes, x_scales, 3 * CHUNK, x_raw[3], 0)

@@ -42,29 +42,35 @@ def tile_picked_recall_none_p_kernel(tc, xT, s_words, s_scales, w1, w2, offs, ou
 
         offsets = keep.tile([P, S // 16], U16, name="offsets")
         store_words = keep.tile([P, T], U32, name="store_words", align_bytes=64)
-        store_scales = keep.tile([P, T], U8, name="store_scales", align_bytes=64)
+        store_scales = keep.tile([P, T], U8, name="store_scales", tag="reused", align_bytes=64)
         w2_raw = keep.tile([P, PACK, M], F32, name="w2_raw", align_bytes=64)
-        w1_raw = keep.tile([P, PACK, M], F32, name="w1_raw", align_bytes=64)
-        x_raw = [keep.tile([P, PACK, CHUNK], F32, name=f"x_raw{c}", align_bytes=64) for c in range(CHUNKS)]
 
-        landed_scales = keep.tile([P, T], U8, name="landed_scales", align_bytes=64)
-        for r in range(4):
-            queue = nc.scalar if r % 2 else nc.sync
-            queue.dma_start(out=landed_scales[r:P:32, :].bitcast(I32), in_=s_scales[0, r:16:4, :].bitcast(I32))
-            if r == 2:
-                nc.sync.dma_start(offsets[:], offs)
-        nc.vector.memset(store_scales[:].bitcast(I32), 0)
-        for q in range(4):
-            live = slice(32 * q, 32 * q + 4)
-            nc.vector.tensor_copy(store_scales[live, :].bitcast(I32), landed_scales[live, :].bitcast(I32))
+        picked_scales = keep.tile([P, S], U8, name="picked_scales", align_bytes=64)
+        mem_scales = keep.tile([P, S], U8, name="mem_scales", align_bytes=64)
+        nc.vector.memset(store_scales[:, 0 : T // 2].bitcast(I32), 0)
+        nc.gpsimd.memset(store_scales[:, T // 2 : T].bitcast(I32), 0)
+        w2_rows = w2.rearrange("(p t) m -> p t m", t=PACK)
+        nc.sync.dma_start(out=w2_raw[:, 0:2, :], in_=w2_rows[:, 0:2, :])
+        nc.sync.dma_start(offsets[:], offs)
+        nc.sync.dma_start(out=store_scales[0:P:8, :].bitcast(I32), in_=s_scales[0].bitcast(I32))
+        nc.sync.dma_start(out=w2_raw[:, 2:4, :], in_=w2_rows[:, 2:4, :])
+        nc.sync.dma_start(out=store_words[:].bitcast(I32), in_=s_words[0].rearrange("p n t -> p (n t)").bitcast(I32))
+        nc.vector.tensor_copy(picked_scales[:], store_scales[:].indirect(offsets[:]))
+        nc.vector.tensor_copy(mem_scales[:].bitcast(I32), picked_scales[:].bitcast(I32))
+        for r in range(1, 4):
+            nc.sync.dma_start(out=mem_scales[r:P:32, :].bitcast(I32), in_=picked_scales[8 * r : P : 32, :].bitcast(I32))
 
+        late = keep.tile([P, PACK * (M + S)], F32, name="late", tag="reused", align_bytes=64)
+        w1_raw = late[:, 0 : PACK * M].rearrange("p (t m) -> p t m", t=PACK)
+        x_raw = [
+            late[:, PACK * (M + c * CHUNK) : PACK * (M + (c + 1) * CHUNK)].rearrange("p (t j) -> p t j", t=PACK)
+            for c in range(CHUNKS)
+        ]
         w1_rows = w1.rearrange("(p t) m -> p t m", t=PACK)
         x_rows = xT.rearrange("(p t) j -> p t j", t=PACK)
-        nc.sync.dma_start(out=w2_raw[:], in_=w2.rearrange("(p t) m -> p t m", t=PACK))
-        nc.sync.dma_start(out=store_words[:].bitcast(I32), in_=s_words[0].rearrange("p n t -> p (n t)").bitcast(I32))
-        nc.sync.dma_start(out=w1_raw[:], in_=w1_rows)
+        nc.sync.dma_start(out=w1_raw, in_=w1_rows)
         for c in range(CHUNKS):
-            nc.sync.dma_start(out=x_raw[c][:], in_=x_rows[:, :, c * CHUNK : (c + 1) * CHUNK])
+            nc.sync.dma_start(out=x_raw[c], in_=x_rows[:, :, c * CHUNK : (c + 1) * CHUNK])
 
         w2_bf = keep.tile([P, M, PACK], BF16, name="w2_bf", align_bytes=64)
         w2_codes = keep.tile([P, M], U32, name="w2_codes", align_bytes=64)
@@ -76,10 +82,9 @@ def tile_picked_recall_none_p_kernel(tc, xT, s_words, s_scales, w1, w2, offs, ou
         x_codes = keep.tile([P, S], U32, name="x_codes", align_bytes=64)
         x_scales = keep.tile([P, S], U8, name="x_scales", align_bytes=64)
         mem_words = keep.tile([P, S], U32, name="mem_words", align_bytes=64)
-        mem_scales = keep.tile([P, S], U8, name="mem_scales", align_bytes=64)
 
-        nc.vector.tensor_copy(mem_scales[:], store_scales[:].indirect(offsets[:]))
-        interleave(nc.scalar.copy, w2_bf[:], w2_raw[:])
+        for t in (0, 2):
+            interleave(nc.scalar.copy, w2_bf[:, :, t : t + 2], w2_raw[:, t : t + 2, :])
         quantize(nc, w2_codes[:], w2_scales[:], w2_bf[:])
         for h in range(S // HALF):
             nc.vector.tensor_copy(

@@ -47,8 +47,7 @@ def tile_picked_recall_none_p_kernel(tc, xT, s_words, s_scales, w1, w2, offs, ou
 
         picked_scales = keep.tile([P, S], U8, name="picked_scales", align_bytes=64)
         mem_scales = keep.tile([P, S], U8, name="mem_scales", align_bytes=64)
-        nc.vector.memset(store_scales[:, 0 : T // 2].bitcast(I32), 0)
-        nc.gpsimd.memset(store_scales[:, T // 2 : T].bitcast(I32), 0)
+        nc.vector.memset(store_scales[:].bitcast(I32), 0)
         w2_rows = w2.rearrange("(p t) m -> p t m", t=PACK)
         nc.sync.dma_start(out=w2_raw[:, 0:2, :], in_=w2_rows[:, 0:2, :])
         nc.sync.dma_start(offsets[:], offs)
@@ -104,7 +103,7 @@ def tile_picked_recall_none_p_kernel(tc, xT, s_words, s_scales, w1, w2, offs, ou
             for a in range(first, first + CHUNK, width):
                 quantize(nc, codes[:, a : a + width], scales[:, a : a + width], bf[:, a : a + width, :])
 
-        def memory_pass(bank, cols, m):
+        def memory_pass(bank, cols, m, start=True):
             rows = slice(m * M_TILE, (m + 1) * M_TILE)
             nc.tensor.matmul_mx(
                 out=bank,
@@ -112,11 +111,11 @@ def tile_picked_recall_none_p_kernel(tc, xT, s_words, s_scales, w1, w2, offs, ou
                 lhsT_scale=w2_scales[:, rows],
                 rhs=mem_words[:, cols].bitcast(FP8X4),
                 rhs_scale=mem_scales[:, cols],
-                start=True,
+                start=start,
                 stop=False,
             )
 
-        def query_pass(bank, cols, m):
+        def query_pass(bank, cols, m, stop=True):
             rows = slice(m * M_TILE, (m + 1) * M_TILE)
             nc.tensor.matmul_mx(
                 out=bank,
@@ -125,7 +124,7 @@ def tile_picked_recall_none_p_kernel(tc, xT, s_words, s_scales, w1, w2, offs, ou
                 rhs=x_codes[:, cols].bitcast(FP8X4),
                 rhs_scale=x_scales[:, cols],
                 start=False,
-                stop=True,
+                stop=stop,
             )
 
         def chunk(c):
@@ -141,8 +140,9 @@ def tile_picked_recall_none_p_kernel(tc, xT, s_words, s_scales, w1, w2, offs, ou
             bank = psum.tile([M_TILE, 2, CHUNK], F32, name=f"bank{b}")
             result = keep.tile([M_TILE, 2, CHUNK], F32, name=f"result{c}{m}", align_bytes=64)
             for i in range(2):
-                memory_pass(bank[:, i, :], chunk(c), m + i)
-                query_pass(bank[:, i, :], chunk(c), m + i)
+                memory_pass(bank[:, i, :], chunk(c), m + i, start=i == 0)
+            for i in range(2):
+                query_pass(bank[:, i, :], chunk(c), m + i, stop=i == 1)
             nc.scalar.copy(result[:], bank[:])
             store(c, m, result)
 
@@ -162,8 +162,9 @@ def tile_picked_recall_none_p_kernel(tc, xT, s_words, s_scales, w1, w2, offs, ou
                 bank = psum.tile([M_TILE, 2, 128], F32, name=f"bank{pair[h]}")
                 cols = slice(c * CHUNK + h * 128, c * CHUNK + (h + 1) * 128)
                 for i in range(2):
-                    memory_pass(bank[:, i, :], cols, m + i)
-                    query_pass(bank[:, i, :], cols, m + i)
+                    memory_pass(bank[:, i, :], cols, m + i, start=i == 0)
+                for i in range(2):
+                    query_pass(bank[:, i, :], cols, m + i, stop=i == 1)
                 copy(result[:, :, h * 128 : (h + 1) * 128], bank[:])
             store(c, m, result)
 

@@ -41,12 +41,12 @@ def tile_picked_recall_none_p_kernel(tc, xT, s_words, s_scales, w1, w2, offs, ou
         psum = ctx.enter_context(tc.psum_pool(name="psum", bufs=1))
 
         offsets = keep.tile([P, S // 16], U16, name="offsets")
-        store_words = keep.tile([P, T], U32, name="store_words", align_bytes=64)
-        store_scales = keep.tile([P, T], U8, name="store_scales", tag="reused", align_bytes=64)
-        w2_raw = keep.tile([P, PACK, M], F32, name="w2_raw", align_bytes=64)
+        store_words = keep.tile([P, T], U32, name="store_words", align_bytes=256)
+        store_scales = keep.tile([P, T], U8, name="store_scales", tag="reused", align_bytes=256)
+        w2_raw = keep.tile([P, PACK, M], F32, name="w2_raw", align_bytes=256)
 
-        picked_scales = keep.tile([P, S], U8, name="picked_scales", align_bytes=64)
-        mem_scales = keep.tile([P, S], U8, name="mem_scales", align_bytes=64)
+        picked_scales = keep.tile([P, S], U8, name="picked_scales", align_bytes=256)
+        mem_scales = keep.tile([P, S], U8, name="mem_scales", align_bytes=256)
         nc.vector.memset(store_scales[:].bitcast(I32), 0)
         w2_rows = w2.rearrange("(p t) m -> p t m", t=PACK)
         nc.sync.dma_start(out=w2_raw[:, 0:2, :], in_=w2_rows[:, 0:2, :])
@@ -59,7 +59,7 @@ def tile_picked_recall_none_p_kernel(tc, xT, s_words, s_scales, w1, w2, offs, ou
         for r in range(1, 4):
             nc.sync.dma_start(out=mem_scales[r:P:32, :].bitcast(I32), in_=picked_scales[8 * r : P : 32, :].bitcast(I32))
 
-        late = keep.tile([P, PACK * (M + S)], F32, name="late", tag="reused", align_bytes=64)
+        late = keep.tile([P, PACK * (M + S)], F32, name="late", tag="reused", align_bytes=256)
         w1_raw = late[:, 0 : PACK * M].rearrange("p (t m) -> p t m", t=PACK)
         x_raw = [
             late[:, PACK * (M + c * CHUNK) : PACK * (M + (c + 1) * CHUNK)].rearrange("p (t j) -> p t j", t=PACK)
@@ -71,16 +71,16 @@ def tile_picked_recall_none_p_kernel(tc, xT, s_words, s_scales, w1, w2, offs, ou
         for c in range(CHUNKS):
             nc.sync.dma_start(out=x_raw[c], in_=x_rows[:, :, c * CHUNK : (c + 1) * CHUNK])
 
-        w2_bf = keep.tile([P, M, PACK], BF16, name="w2_bf", align_bytes=64)
-        w2_codes = keep.tile([P, M], U32, name="w2_codes", align_bytes=64)
-        w2_scales = keep.tile([P, M], U8, name="w2_scales", align_bytes=64)
-        w1_bf = keep.tile([P, M, PACK], BF16, name="w1_bf", align_bytes=64)
-        w1_codes = keep.tile([P, M], U32, name="w1_codes", align_bytes=64)
-        w1_scales = keep.tile([P, M], U8, name="w1_scales", align_bytes=64)
-        x_bf = keep.tile([P, S, PACK], BF16, name="x_bf", align_bytes=64)
-        x_codes = keep.tile([P, S], U32, name="x_codes", align_bytes=64)
-        x_scales = keep.tile([P, S], U8, name="x_scales", align_bytes=64)
-        mem_words = keep.tile([P, S], U32, name="mem_words", align_bytes=64)
+        w2_bf = keep.tile([P, M, PACK], BF16, name="w2_bf", align_bytes=256)
+        w2_codes = keep.tile([P, M], U32, name="w2_codes", align_bytes=256)
+        w2_scales = keep.tile([P, M], U8, name="w2_scales", align_bytes=256)
+        w1_bf = keep.tile([P, M, PACK], BF16, name="w1_bf", align_bytes=256)
+        w1_codes = keep.tile([P, M], U32, name="w1_codes", align_bytes=256)
+        w1_scales = keep.tile([P, M], U8, name="w1_scales", align_bytes=256)
+        x_bf = keep.tile([P, S, PACK], BF16, name="x_bf", align_bytes=256)
+        x_codes = keep.tile([P, S], U32, name="x_codes", align_bytes=256)
+        x_scales = keep.tile([P, S], U8, name="x_scales", align_bytes=256)
+        mem_words = keep.tile([P, S], U32, name="mem_words", align_bytes=256)
 
         for t in (0, 2):
             interleave(nc.scalar.copy, w2_bf[:, :, t : t + 2], w2_raw[:, t : t + 2, :])
@@ -138,7 +138,7 @@ def tile_picked_recall_none_p_kernel(tc, xT, s_words, s_scales, w1, w2, offs, ou
 
         def shared_block(c, m, b):
             bank = psum.tile([M_TILE, 2, CHUNK], F32, name=f"bank{b}")
-            result = keep.tile([M_TILE, 2, CHUNK], F32, name=f"result{c}{m}", align_bytes=64)
+            result = keep.tile([M_TILE, 2, CHUNK], F32, name=f"result{c}{m}", align_bytes=256)
             for i in range(2):
                 memory_pass(bank[:, i, :], chunk(c), m + i, start=i == 0)
             for i in range(2):
@@ -148,7 +148,7 @@ def tile_picked_recall_none_p_kernel(tc, xT, s_words, s_scales, w1, w2, offs, ou
 
         def split_block(c, m, pair, second_copy):
             banks = [psum.tile([M_TILE, CHUNK], F32, name=f"bank{b}") for b in pair]
-            result = keep.tile([M_TILE, 2, CHUNK], F32, name=f"result{c}{m}", align_bytes=64)
+            result = keep.tile([M_TILE, 2, CHUNK], F32, name=f"result{c}{m}", align_bytes=256)
             for i in range(2):
                 memory_pass(banks[i][:], chunk(c), m + i)
             for i, copy in enumerate((nc.scalar.copy, second_copy)):
@@ -157,7 +157,7 @@ def tile_picked_recall_none_p_kernel(tc, xT, s_words, s_scales, w1, w2, offs, ou
             store(c, m, result)
 
         def halved_block(c, m, pair, second_copy):
-            result = keep.tile([M_TILE, 2, CHUNK], F32, name=f"result{c}{m}", align_bytes=64)
+            result = keep.tile([M_TILE, 2, CHUNK], F32, name=f"result{c}{m}", align_bytes=256)
             for h, copy in enumerate((nc.scalar.copy, second_copy)):
                 bank = psum.tile([M_TILE, 2, 128], F32, name=f"bank{pair[h]}")
                 cols = slice(c * CHUNK + h * 128, c * CHUNK + (h + 1) * 128)

@@ -180,6 +180,6 @@ def tile_picked_recall_none_p_kernel(tc, xT, s_words, s_scales, w1, w2, offs, ou
         shared_block(1, 2, 5)
         prepare(x_bf, x_codes, x_scales, 3 * CHUNK, x_raw[3], 0)
         halved_block(2, 0, (0, 1), nc.scalar.copy)
-        shared_block(2, 2, 6)
+        shared_block(2, 2, 2)
         halved_block(3, 0, (3, 4), nc.vector.tensor_copy)
-        split_block(3, 2, (7, 2), nc.vector.tensor_copy)
+        split_block(3, 2, (6, 5), nc.vector.tensor_copy)

from contextlib import ExitStack

import concourse.mybir as mybir

K, T, S, M = 512, 4096, 1024, 512
FLOPS = 2 * 2 * K * M * S

F32 = mybir.dt.float32
BF16 = mybir.dt.bfloat16
I32 = mybir.dt.int32
U32 = mybir.dt.uint32
U16 = mybir.dt.uint16
U8 = mybir.dt.uint8
FP8X4 = mybir.dt.float8_e4m3fn_x4

P = 128
PACK = 4
M_TILE = 128
M_TILES = M // M_TILE
CHUNK = 256
CHUNKS = S // CHUNK
HALF = 512


def interleave(copy, grouped, raw):
    copy(grouped.rearrange("p (c i) t -> p c t i", i=2), raw.rearrange("p t (c i) -> p c t i", i=2))


def quantize(nc, codes, scales, grouped):
    nc.vector.quantize_mx(
        out=codes.bitcast(FP8X4),
        scales=scales,
        in_=grouped.rearrange("p c t -> p (c t)"),
    )


def tile_picked_recall_none_p_kernel(tc, xT, s_words, s_scales, w1, w2, offs, out):
    nc = tc.nc
    with ExitStack() as ctx:
        keep = ctx.enter_context(tc.tile_pool(name="keep", bufs=1))
        psum = ctx.enter_context(tc.psum_pool(name="psum", bufs=1))

        offsets = keep.tile([P, S // 16], U16, name="offsets")
        store_words = keep.tile([P, T], U32, name="store_words", align_bytes=256)
        store_scales = keep.tile([P, T], U8, name="store_scales", tag="reused", align_bytes=256)
        w2_raw = keep.tile([P, PACK, M], F32, name="w2_raw", align_bytes=256)

        picked_scales = keep.tile([P, S], U8, name="picked_scales", align_bytes=256)
        mem_scales = keep.tile([P, S], U8, name="mem_scales", align_bytes=256)
        nc.vector.memset(store_scales[:].bitcast(I32), 0)
        w2_rows = w2.rearrange("(p t) m -> p t m", t=PACK)
        nc.sync.dma_start(out=w2_raw[:, 0:2, :], in_=w2_rows[:, 0:2, :])
        nc.sync.dma_start(offsets[:], offs)
        nc.sync.dma_start(out=store_scales[0:P:8, :].bitcast(I32), in_=s_scales[0].bitcast(I32))
        nc.sync.dma_start(out=w2_raw[:, 2:4, :], in_=w2_rows[:, 2:4, :])
        nc.sync.dma_start(out=store_words[:].bitcast(I32), in_=s_words[0].rearrange("p n t -> p (n t)").bitcast(I32))
        nc.vector.tensor_copy(picked_scales[:], store_scales[:].indirect(offsets[:]))
        nc.vector.tensor_copy(mem_scales[:].bitcast(I32), picked_scales[:].bitcast(I32))
        for r in range(1, 4):
            nc.sync.dma_start(out=mem_scales[r:P:32, :].bitcast(I32), in_=picked_scales[8 * r : P : 32, :].bitcast(I32))

        late = keep.tile([P, PACK * (M + S)], F32, name="late", tag="reused", align_bytes=256)
        w1_raw = late[:, 0 : PACK * M].rearrange("p (t m) -> p t m", t=PACK)
        x_raw = [
            late[:, PACK * (M + c * CHUNK) : PACK * (M + (c + 1) * CHUNK)].rearrange("p (t j) -> p t j", t=PACK)
            for c in range(CHUNKS)
        ]
        w1_rows = w1.rearrange("(p t) m -> p t m", t=PACK)
        x_rows = xT.rearrange("(p t) j -> p t j", t=PACK)
        nc.sync.dma_start(out=w1_raw, in_=w1_rows)
        for c in range(CHUNKS):
            nc.sync.dma_start(out=x_raw[c], in_=x_rows[:, :, c * CHUNK : (c + 1) * CHUNK])

        w2_bf = keep.tile([P, M, PACK], BF16, name="w2_bf", align_bytes=256)
        w2_codes = keep.tile([P, M], U32, name="w2_codes", align_bytes=256)
        w2_scales = keep.tile([P, M], U8, name="w2_scales", align_bytes=256)
        w1_bf = keep.tile([P, M, PACK], BF16, name="w1_bf", align_bytes=256)
        w1_codes = keep.tile([P, M], U32, name="w1_codes", align_bytes=256)
        w1_scales = keep.tile([P, M], U8, name="w1_scales", align_bytes=256)
        x_bf = keep.tile([P, S, PACK], BF16, name="x_bf", align_bytes=256)
        x_codes = keep.tile([P, S], U32, name="x_codes", align_bytes=256)
        x_scales = keep.tile([P, S], U8, name="x_scales", align_bytes=256)
        mem_words = keep.tile([P, S], U32, name="mem_words", align_bytes=256)

        for t in (0, 2):
            interleave(nc.scalar.copy, w2_bf[:, :, t : t + 2], w2_raw[:, t : t + 2, :])
        quantize(nc, w2_codes[:], w2_scales[:], w2_bf[:])
        for h in range(S // HALF):
            nc.vector.tensor_copy(
                mem_words[:, h * HALF : (h + 1) * HALF],
                store_words[:].indirect(offsets[:, h * HALF // 16 : (h + 1) * HALF // 16]),
            )

        def prepare(bf, codes, scales, first, raw, scalar_share):
            share = CHUNK - scalar_share
            cuts = [0, share] if share <= 128 else [0, 128, share]
            for a, b in zip(cuts, cuts[1:]):
                if b > a:
                    interleave(nc.vector.tensor_copy, bf[:, first + a : first + b, :], raw[:, :, a:b])
            if scalar_share:
                interleave(nc.scalar.copy, bf[:, first + share : first + CHUNK, :], raw[:, :, share:CHUNK])
            width = 128 if share > 128 or bf is w1_bf else CHUNK
            for a in range(first, first + CHUNK, width):
                quantize(nc, codes[:, a : a + width], scales[:, a : a + width], bf[:, a : a + width, :])

        def memory_pass(bank, cols, m, start=True):
            rows = slice(m * M_TILE, (m + 1) * M_TILE)
            nc.tensor.matmul_mx(
                out=bank,
                lhsT=w2_codes[:, rows].bitcast(FP8X4),
                lhsT_scale=w2_scales[:, rows],
                rhs=mem_words[:, cols].bitcast(FP8X4),
                rhs_scale=mem_scales[:, cols],
                start=start,
                stop=False,
            )

        def query_pass(bank, cols, m, stop=True):
            rows = slice(m * M_TILE, (m + 1) * M_TILE)
            nc.tensor.matmul_mx(
                out=bank,
                lhsT=w1_codes[:, rows].bitcast(FP8X4),
                lhsT_scale=w1_scales[:, rows],
                rhs=x_codes[:, cols].bitcast(FP8X4),
                rhs_scale=x_scales[:, cols],
                start=False,
                stop=stop,
            )

        def chunk(c):
            return slice(c * CHUNK, (c + 1) * CHUNK)

        out_rows = out.rearrange("(m p) j -> p m j", p=M_TILE)

        def store(c, m, result):
            queue = nc.scalar if (c, m) == (CHUNKS - 1, 2) else nc.sync
            queue.dma_start(out=out_rows[:, m : m + 2, c * CHUNK : (c + 1) * CHUNK], in_=result[:])

        def shared_block(c, m, b):
            bank = psum.tile([M_TILE, 2, CHUNK], F32, name=f"bank{b}")
            result = keep.tile([M_TILE, 2, CHUNK], F32, name=f"result{c}{m}", align_bytes=256)
            for i in range(2):
                memory_pass(bank[:, i, :], chunk(c), m + i, start=i == 0)
            for i in range(2):
                query_pass(bank[:, i, :], chunk(c), m + i, stop=i == 1)
            nc.scalar.copy(result[:], bank[:])
            store(c, m, result)

        def split_block(c, m, pair, second_copy):
            banks = [psum.tile([M_TILE, CHUNK], F32, name=f"bank{b}") for b in pair]
            result = keep.tile([M_TILE, 2, CHUNK], F32, name=f"result{c}{m}", align_bytes=256)
            for i in range(2):
                memory_pass(banks[i][:], chunk(c), m + i)
            for i, copy in enumerate((nc.scalar.copy, second_copy)):
                query_pass(banks[i][:], chunk(c), m + i)
                copy(result[:, i, :], banks[i][:])
            store(c, m, result)

        def halved_block(c, m, pair, second_copy):
            result = keep.tile([M_TILE, 2, CHUNK], F32, name=f"result{c}{m}", align_bytes=256)
            for h, copy in enumerate((nc.scalar.copy, second_copy)):
                bank = psum.tile([M_TILE, 2, 128], F32, name=f"bank{pair[h]}")
                cols = slice(c * CHUNK + h * 128, c * CHUNK + (h + 1) * 128)
                for i in range(2):
                    memory_pass(bank[:, i, :], cols, m + i, start=i == 0)
                for i in range(2):
                    query_pass(bank[:, i, :], cols, m + i, stop=i == 1)
                copy(result[:, :, h * 128 : (h + 1) * 128], bank[:])
            store(c, m, result)

        prepare(w1_bf, w1_codes, w1_scales, 0, w1_raw[:, :, 0:CHUNK], 0)
        interleave(nc.scalar.copy, w1_bf[:, CHUNK:M, :], w1_raw[:, :, CHUNK:M])
        prepare(x_bf, x_codes, x_scales, 0, x_raw[0], 96)
        quantize(nc, w1_codes[:, CHUNK:M], w1_scales[:, CHUNK:M], w1_bf[:, CHUNK:M, :])
        prepare(x_bf, x_codes, x_scales, CHUNK, x_raw[1], 96)
        split_block(0, 0, (0, 1), nc.scalar.copy)
        shared_block(0, 2, 2)
        prepare(x_bf, x_codes, x_scales, 2 * CHUNK, x_raw[2], 48)
        split_block(1, 0, (3, 4), nc.scalar.copy)
        shared_block(1, 2, 5)
        prepare(x_bf, x_codes, x_scales, 3 * CHUNK, x_raw[3], 0)
        halved_block(2, 0, (0, 1), nc.scalar.copy)
        shared_block(2, 2, 2)
        halved_block(3, 0, (3, 4), nc.vector.tensor_copy)
        split_block(3, 2, (6, 5), nc.vector.tensor_copy)
